import numpy as np
import ml_dtypes


def mxq(x, axis, fmt="e4m3"):
    dtype, down = {"e4m3": (ml_dtypes.float8_e4m3fn, 7), "e5m2": (ml_dtypes.float8_e5m2, 14)}[fmt]
    v = np.moveaxis(np.asarray(x, np.float32).astype(ml_dtypes.bfloat16).astype(np.float64), axis, -1)
    blocks = v.reshape(v.shape[:-1] + (-1, 32))
    amax = np.abs(blocks).max(-1, keepdims=True)
    byte = np.maximum(np.where(amax > 0, np.frexp(amax)[1] - 1 + 127, 0) - down, 1)
    scale = np.exp2(byte - 127.0)
    codes = (blocks / scale).astype(np.float32).astype(dtype).astype(np.float64)
    return np.moveaxis((codes * scale).reshape(v.shape), -1, axis)


WIDE = False


def mx_kscale(k):
    if not WIDE:
        return np.ones(k)
    levels = np.array([10, -10, 5, -5, 0])
    if k % 512:
        return np.exp2(np.random.permutation(np.resize(levels, k // 32))).repeat(32)
    a = np.empty((k // 512, 16))
    for p in range(k // 512):
        a[p, :8] = np.random.permutation(np.resize(levels, 8))
        for g in range(8):
            far = levels[np.abs(levels - a[p, g]) >= 10]
            a[p, g + 8] = far[np.random.randint(len(far))]
    return np.exp2(a.ravel()).repeat(32)


def f64(x):
    return np.asarray(x).astype(np.float64)


def striped(idx):
    return np.tile(idx.reshape(-1, 16).T, (8, 1)).astype(np.uint16)


def unstriped(offs):
    return offs[:16].T.reshape(-1).astype(np.int64)


def pack_weight(w):
    k, n = w.shape
    w = f64(np.asarray(w, np.float32).astype(ml_dtypes.bfloat16)).reshape(k // 32, 32, n)
    amax = np.abs(w).max(1)
    byte = np.clip(np.where(amax > 0, np.frexp(amax)[1] - 1 + 127 - 7, 1), 1, 254)
    scaled = (w * np.exp2(127.0 - byte)[:, None, :]).reshape(k, n).astype(np.float32)
    words = np.ascontiguousarray(scaled.reshape(k // 512, 128, 4, n).transpose(0, 1, 3, 2)).astype(ml_dtypes.float8_e4m3fn).view(np.uint8)
    return words, np.ascontiguousarray(byte.astype(np.uint8).reshape(k // 512, 16, n))


def unpack_weight(words, scales):
    g, p, n, _ = words.shape
    vals = np.ascontiguousarray(words).view(ml_dtypes.float8_e4m3fn).astype(np.float64) * np.repeat(np.exp2(scales.astype(np.float64) - 127.0), 8, axis=1)[..., None]
    return vals.transpose(0, 1, 3, 2).reshape(g * 512, n)


E2M1 = np.array([0.0, 0.5, 1.0, 1.5, 2.0, 3.0, 4.0, 6.0, -0.0, -0.5, -1.0, -1.5, -2.0, -3.0, -4.0, -6.0])


def pack_fp4(w):
    k, n = w.shape
    w = f64(np.asarray(w, np.float32).astype(ml_dtypes.bfloat16)).reshape(k // 32, 32, n)
    amax = np.abs(w).max(1)
    mant, ex = np.frexp(amax / 6.0)
    byte = np.clip(np.where(amax > 0, np.where(mant > 0.5, ex, ex - 1) + 127, 1), 1, 254)
    scaled = (w * np.exp2(127.0 - byte)[:, None, :]).reshape(k, n).astype(np.float32)
    c = np.ascontiguousarray(scaled.reshape(k // 512, 128, 4, n).transpose(0, 1, 3, 2)).astype(ml_dtypes.float4_e2m1fn).view(np.uint8) & 0xF
    words = (c[..., 0::2] | (c[..., 1::2] << 4)).reshape(k // 512, 128, 2 * n)
    return np.ascontiguousarray(words), np.ascontiguousarray(byte.astype(np.uint8).reshape(k // 512, 16, n))


def unpack_fp4(words, scales):
    g, _, n = scales.shape
    words = np.ascontiguousarray(words).reshape(g, 128, n, 2)
    nib = np.empty((g, 128, n, 4), np.uint8)
    nib[..., 0::2] = words & 0xF
    nib[..., 1::2] = words >> 4
    vals = E2M1[nib] * np.repeat(np.exp2(scales.astype(np.float64) - 127.0), 8, axis=1)[..., None]
    return vals.transpose(0, 1, 3, 2).reshape(g * 512, n)


K, T, S, N, H = 1024, 2048, 512, 256, 512


def setup_inputs():
    n = np.random.standard_normal
    s = mx_kscale(K)[:, None]
    u = mx_kscale(H)
    packed_xT = pack_weight(n((K, T)) * s)
    packed_w1 = pack_fp4(n((K, H)) / np.sqrt(K) / s)
    packed_w2 = pack_fp4(n((K, H)) / np.sqrt(K) / s)
    packed_w3 = pack_fp4(n((H, N)) / np.sqrt(H) / u[:, None])
    return {
        "x_words": packed_xT[0],
        "x_scales": packed_xT[1],
        "w1_words": packed_w1[0],
        "w1_scales": packed_w1[1],
        "w2_words": packed_w2[0],
        "w2_scales": packed_w2[1],
        "intf": (np.random.uniform(0.2, 0.8, (H, S))).astype(np.float32),
        "age": (np.random.uniform(0.3, 2.5, (H, S))).astype(np.float32),
        "unit": (np.random.uniform(0.6, 1.4, (H, 1)) * u[:, None]).astype(np.float32),
        "w3_words": packed_w3[0],
        "w3_scales": packed_w3[1],
        "offs": striped(np.random.permutation(T)[:S]),
        "off": striped(np.random.permutation(S)),
    }


def reference(x_words, x_scales, w1_words, w1_scales, w2_words, w2_scales, intf, age, unit, w3_words, w3_scales, offs, off):
    xq = unpack_weight(x_words, x_scales)[:, unstriped(offs)]
    qi = unpack_fp4(w2_words, w2_scales).T @ xq
    init = np.exp(0.9 * np.tanh(qi))
    di = unpack_fp4(w1_words, w1_scales).T @ xq
    dec = 0.5 * (np.log(np.exp(di) + 1.0)) + 0.1
    do = dec[:, unstriped(off)]
    itf = do * f64(intf)
    strc = np.sqrt((dec + itf) * f64(age))
    rate = init * np.exp(-1.0 * strc)
    ro = rate[:, unstriped(off)]
    hid = f64(unit) * (rate - (0.4 * ro))
    return unpack_fp4(w3_words, w3_scales).T @ mxq(hid, 0, "e4m3")

@@ -1,0 +1,230 @@
+import math
+from contextlib import ExitStack
+
+import concourse.mybir as mybir
+from concourse.masks import make_identity
+
+K, T, S, N, H = 1024, 2048, 512, 256, 512
+FLOPS = 2 * (2 * K * H * S + H * N * S)
+
+F32, BF16 = mybir.dt.float32, mybir.dt.bfloat16
+I32, U32, U16, U8 = mybir.dt.int32, mybir.dt.uint32, mybir.dt.uint16, mybir.dt.uint8
+FP8X4, FP4X4 = mybir.dt.float8_e4m3fn_x4, mybir.dt.float4_e2m1fn_x4
+ALU = mybir.AluOpType
+ACT = mybir.ActivationFunctionType
+
+P = 128
+PACK = 4
+PASSES = K // (P * PACK)
+QUADS = 4
+BLOCKS = S // P
+WINDOW = 704
+EXP_CAP = 2.0**56
+CHUNKS = 4
+KIB = 1024
+
+
+def load_scale_rows(queue, plane, scales):
+    for q in range(QUADS):
+        queue.dma_start(
+            out=plane[32 * q : 32 * q + 4].bitcast(I32),
+            in_=scales[:, 4 * q : 4 * q + 4, :].rearrange("o r c -> r o c").bitcast(I32),
+        )
+
+
+def load_words(queue, tile, words):
+    queue.dma_start(out=tile.bitcast(I32), in_=words.bitcast(I32))
+
+
+def tile_picked_yarpsd_str_p_kernel(
+    tc, x_words, x_scales, w1_words, w1_scales, w2_words, w2_scales, intf, age, unit, w3_words, w3_scales, offs, off, out
+):
+    nc = tc.nc
+    with ExitStack() as ctx:
+        keep = ctx.enter_context(tc.tile_pool(name="keep", bufs=1))
+        shared = ctx.enter_context(tc.tile_pool(name="shared", bufs=1))
+        psum = ctx.enter_context(tc.psum_pool(name="psum", bufs=1))
+
+        offs_sb = keep.tile([P, S // 16], U16, name="offs_sb")
+        off_sb = keep.tile([P, S // 16], U16, name="off_sb")
+        xs_table = shared.tile([P, PASSES, T], U8, name="xs_table", offset=0, align_bytes=64)
+        x_table = [
+            shared.tile([P, T], I32, name="x_table0", offset=4 * KIB, align_bytes=64),
+            shared.tile([P, T], I32, name="x_table1", offset=16 * KIB, align_bytes=64),
+        ]
+        w2_sb = shared.tile([P, PASSES, 2 * H], U8, name="w2_sb", offset=0, align_bytes=64)
+        w1s_dealt = shared.tile([P, PASSES, H], U8, name="w1s_dealt", offset=8 * KIB, align_bytes=64)
+        intf_sb = [
+            shared.tile([P, 2, S], F32, name="intf0", offset=4 * KIB, align_bytes=64),
+            shared.tile([P, 2, S], F32, name="intf1", offset=16 * KIB, align_bytes=64),
+        ]
+        age_sb = [
+            shared.tile([P, 2, S], F32, name="age0", offset=11 * KIB, align_bytes=64),
+            shared.tile([P, 2, S], F32, name="age1", offset=20 * KIB, align_bytes=64),
+        ]
+        w1_raw = keep.tile([P, PASSES, 2 * H], U8, name="w1_raw")
+        w1_dealt = keep.tile([P, PASSES, 2 * H], U8, name="w1_dealt", align_bytes=64)
+        w1s_raw = shared.tile([P, PASSES, H], U8, name="w1s_raw", offset=24 * KIB, align_bytes=64)
+        w2s_sb = keep.tile([P, PASSES, H], U8, name="w2s_sb", align_bytes=64)
+        w3_sb = keep.tile([P, 2 * N], U8, name="w3_sb", align_bytes=64)
+        w3s_sb = keep.tile([P, 1, N], U8, name="w3s_sb", align_bytes=64)
+        unit_sb = keep.tile([P, PACK], F32, name="unit_sb")
+        ident = keep.tile([P, P], F32, name="ident")
+        windows = [keep.tile([P, WINDOW], F32, name=f"window{t}") for t in range(PACK)]
+
+        nc.vector.memset(w1s_raw[:].bitcast(I32), 0)
+        nc.vector.memset(xs_table[:].bitcast(I32), 0)
+        nc.vector.memset(w2s_sb[:].bitcast(I32), 0)
+        nc.vector.memset(w3s_sb[:].bitcast(I32), 0)
+        for t in range(PACK):
+            nc.vector.memset(windows[t][:, S:], 0.0)
+
+        nc.sync.dma_start(offs_sb[:], offs)
+        for o in range(PASSES):
+            load_words(nc.sync, x_table[o][:], x_words[o].rearrange("p c r -> p (c r)"))
+        nc.sync.dma_start(off_sb[:], off)
+        load_scale_rows(nc.sync, xs_table, x_scales)
+        load_scale_rows(nc.sync, w2s_sb, w2_scales)
+        load_words(nc.gpsimd, w1_raw[:], w1_words.rearrange("o p b -> p o b"))
+        load_scale_rows(nc.gpsimd, w1s_raw, w1_scales)
+        make_identity(nc, ident[:])
+        nc.gpsimd.dma_start(out=unit_sb[:], in_=unit.rearrange("(p t) o -> p (t o)", t=PACK))
+        load_words(nc.gpsimd, w3_sb[:], w3_words[0])
+        load_scale_rows(nc.gpsimd, w3s_sb, w3_scales)
+
+        nc.scalar.copy(
+            out=w1_dealt[:].bitcast(U16).rearrange("p o (t m) -> p o t m", t=PACK),
+            in_=w1_raw[:].bitcast(U16).rearrange("p o (m t) -> p o t m", t=PACK),
+        )
+        x_codes = [
+            keep.tile([P, S], U32, name="x_codes0", align_bytes=64),
+            shared.tile([P, S], U32, name="x_codes1", offset=24 * KIB, align_bytes=64),
+        ]
+        x_plane = [keep.tile([P, S], U8, name=f"x_plane{o}", align_bytes=64) for o in range(PASSES)]
+        for o in range(PASSES):
+            nc.vector.tensor_copy(x_plane[o][:], xs_table[:, o, :].indirect(offs_sb[:]))
+        nc.vector.tensor_copy(x_codes[0][:], x_table[0][:].bitcast(U32).indirect(offs_sb[:]))
+        nc.vector.tensor_copy(
+            out=w1s_dealt[:].rearrange("p o (t m) -> p o t m", t=PACK),
+            in_=w1s_raw[:].rearrange("p o (m t) -> p o t m", t=PACK),
+        )
+        nc.vector.tensor_copy(x_codes[1][:], x_table[1][:].bitcast(U32).indirect(offs_sb[:]))
+
+        load_words(nc.sync, w2_sb[:], w2_words.rearrange("o p b -> p o b"))
+        for h in range(2):
+            nc.sync.dma_start(out=intf_sb[h][:], in_=intf.rearrange("(p t) j -> p t j", t=PACK)[:, 2 * h : 2 * h + 2, :])
+            nc.sync.dma_start(out=age_sb[h][:], in_=age.rearrange("(p t) j -> p t j", t=PACK)[:, 2 * h : 2 * h + 2, :])
+
+        di = [psum.tile([P, S], F32, name=f"di{t}", tag=f"tile_bank{t}") for t in range(PACK)]
+        for o, t in [(0, 0), (0, 1), (1, 0), (1, 1), (0, 2), (1, 2), (0, 3), (1, 3)]:
+            nc.tensor.matmul_mx(
+                out=di[t][:],
+                lhsT=w1_dealt[:, o, 2 * P * t : 2 * P * (t + 1)].bitcast(FP4X4),
+                lhsT_scale=w1s_dealt[:, o, P * t : P * (t + 1)],
+                rhs=x_codes[o][:].bitcast(FP8X4),
+                rhs_scale=x_plane[o][:],
+                start=(o == 0),
+                stop=(o == PASSES - 1),
+            )
+        qi_t = [psum.tile([P, H], F32, name=f"qi_t{u}", tag=f"block_bank{u}") for u in range(BLOCKS)]
+        for u in range(BLOCKS):
+            for o in range(PASSES):
+                nc.tensor.matmul_mx(
+                    out=qi_t[u][:],
+                    lhsT=x_codes[o][:, P * u : P * (u + 1)].bitcast(FP8X4),
+                    lhsT_scale=x_plane[o][:, P * u : P * (u + 1)],
+                    rhs=w2_sb[:, o, :].bitcast(FP4X4),
+                    rhs_scale=w2s_sb[:, o, :],
+                    start=(o == 0),
+                    stop=(o == PASSES - 1),
+                )
+
+        soft = keep.tile([P, PACK, S], F32, name="soft")
+        tanh_t = keep.tile([P, PACK, BLOCKS, P], F32, name="tanh_t")
+        own = keep.tile([P, PACK, S], F32, name="own")
+        other = keep.tile([P, PACK, S], F32, name="other")
+        strc_t = keep.tile([P, PACK, S], F32, name="strc_t")
+        for t in range(PACK):
+            nc.scalar.activation(soft[:, t, :], di[t][:], ACT.Exp)
+        for u in range(BLOCKS):
+            nc.scalar.activation(tanh_t[:, :, u, :], qi_t[u][:].rearrange("j (p t) -> j t p", t=PACK), ACT.Tanh, scale=-1.0)
+        nc.vector.tensor_scalar(soft[:], soft[:], EXP_CAP, 1.0, ALU.min, ALU.add)
+        for h in range(2):
+            nc.vector.tensor_tensor(intf_sb[h][:], intf_sb[h][:], age_sb[h][:], ALU.mult)
+        for t in range(PACK):
+            nc.scalar.activation(soft[:, t, :], soft[:, t, :], ACT.Ln, scale=math.exp(0.2))
+        for t in range(PACK):
+            nc.vector.scalar_tensor_tensor(windows[t][:, :S], di[t][:], 0.2, soft[:, t, :], ALU.add, ALU.max)
+        for t in range(1, PACK):
+            nc.scalar.activation(other[:, t, :], windows[t][:].indirect(off_sb[:]), ACT.Copy)
+
+        def add_transposed(bank, first, second):
+            for n, src in enumerate((first, second)):
+                for u in range(BLOCKS):
+                    nc.tensor.matmul(
+                        bank[:, P * u : P * (u + 1)],
+                        src[:, P * u : P * (u + 1)],
+                        ident[:],
+                        is_transpose=True,
+                        start=(n == 0 and u == 0),
+                        stop=(n == 1 and u == BLOCKS - 1),
+                    )
+
+        args = {}
+        for t in range(PACK):
+            intf_age = intf_sb[t // 2][:, t % 2, :]
+            nc.vector.tensor_tensor(own[:, t, :], windows[t][:, :S], age_sb[t // 2][:, t % 2, :], ALU.mult)
+            if t == 0:
+                nc.vector.tensor_tensor(other[:, t, :], windows[t][:].indirect(off_sb[:]), intf_age, ALU.mult)
+            else:
+                nc.vector.tensor_tensor(other[:, t, :], other[:, t, :], intf_age, ALU.mult)
+            z_t = psum.tile([P, S], F32, name=f"z_t{t}", tag=f"tile_bank{t}")
+            add_transposed(z_t, own[:, t, :], other[:, t, :])
+            nc.scalar.activation(strc_t[:, t, :], z_t[:], ACT.Sqrt, scale=0.5 / 0.81)
+        tanh_rows = [tanh_t[:, t].rearrange("j u p -> j (u p)") for t in range(PACK)]
+        for t, bank in [(1, 1), (2, 2), (0, 3), (3, 0)]:
+            arg = psum.tile([P, S], F32, name=f"arg{t}", tag=f"tile_bank{bank}")
+            add_transposed(arg, tanh_rows[t], strc_t[:, t, :])
+            args[t] = arg
+        rate = [soft[:, 0, :], strc_t[:, 0, :], tanh_rows[0], soft[:, 3, :]]
+        for t in range(PACK):
+            nc.scalar.activation(rate[t], args[t][:], ACT.Exp, scale=-0.9)
+            if t == 0:
+                nc.vector.tensor_scalar(windows[t][:, :S], rate[t], unit_sb[:, t : t + 1], -0.4, ALU.mult, ALU.mult)
+                nc.vector.tensor_copy(other[:, t, :], windows[t][:].indirect(off_sb[:]))
+            nc.vector.tensor_scalar(own[:, t, :], rate[t], unit_sb[:, t : t + 1], None, ALU.mult)
+
+        cw = S // CHUNKS
+        hid = keep.tile([P, S, PACK], BF16, name="hid", align_bytes=64)
+        hid_codes = keep.tile([P, S], U32, name="hid_codes", align_bytes=64)
+        hid_plane = keep.tile([P, S], U8, name="hid_plane", align_bytes=64)
+        staged = keep.tile([P, N // P, S], F32, name="staged")
+        for c in range(CHUNKS):
+            cols = slice(c * cw, (c + 1) * cw)
+            entries = off_sb[:, c * cw // 16 : (c + 1) * cw // 16]
+            for t in range(1, PACK):
+                nc.scalar.activation(other[:, t, cols], own[:, t, :].indirect(entries), ACT.Copy, scale=-0.4)
+            nc.vector.tensor_tensor(
+                hid[:, cols, :].rearrange("p (c i) t -> p c t i", i=4),
+                other[:, :, cols].rearrange("p t (c i) -> p c t i", i=4),
+                own[:, :, cols].rearrange("p t (c i) -> p c t i", i=4),
+                ALU.add,
+            )
+            nc.vector.quantize_mx(
+                out=hid_codes[:, cols].bitcast(FP8X4),
+                scales=hid_plane[:, cols],
+                in_=hid[:, cols, :].rearrange("p j t -> p (j t)"),
+            )
+            acc = psum.tile([P, N // P, cw], F32, name=f"acc{c}", tag=f"block_bank{c}")
+            for m in range(N // P):
+                nc.tensor.matmul_mx(
+                    out=acc[:, m, :],
+                    lhsT=w3_sb[:, 2 * P * m : 2 * P * (m + 1)].bitcast(FP4X4),
+                    lhsT_scale=w3s_sb[:, 0, P * m : P * (m + 1)],
+                    rhs=hid_codes[:, cols].bitcast(FP8X4),
+                    rhs_scale=hid_plane[:, cols],
+                    start=True,
+                    stop=True,
+                )
+            nc.vector.tensor_copy(out=staged[:, :, cols], in_=acc[:])
+            nc.sync.dma_start(out=out.rearrange("(m p) j -> p m j", p=P)[:, :, cols], in_=staged[:, :, cols])

@@ -25,10 +25,10 @@ KIB = 1024
 
 
 def load_scale_rows(queue, plane, scales):
-    for q in range(QUADS):
+    for r in range(4):
         queue.dma_start(
-            out=plane[32 * q : 32 * q + 4].bitcast(I32),
-            in_=scales[:, 4 * q : 4 * q + 4, :].rearrange("o r c -> r o c").bitcast(I32),
+            out=plane[r:P:32].bitcast(I32),
+            in_=scales.rearrange("o (q r) c -> r q o c", r=4)[r].bitcast(I32),
         )
 
 
@@ -47,62 +47,68 @@ def tile_picked_yarpsd_str_p_kernel(
 
         offs_sb = keep.tile([P, S // 16], U16, name="offs_sb")
         off_sb = keep.tile([P, S // 16], U16, name="off_sb")
-        xs_table = shared.tile([P, PASSES, T], U8, name="xs_table", offset=0, align_bytes=64)
+        xs_table = shared.tile([P, T], U8, name="xs_table", offset=0, align_bytes=64)
         x_table = [
             shared.tile([P, T], I32, name="x_table0", offset=4 * KIB, align_bytes=64),
             shared.tile([P, T], I32, name="x_table1", offset=16 * KIB, align_bytes=64),
         ]
-        w2_sb = shared.tile([P, PASSES, 2 * H], U8, name="w2_sb", offset=0, align_bytes=64)
-        w1s_dealt = shared.tile([P, PASSES, H], U8, name="w1s_dealt", offset=8 * KIB, align_bytes=64)
+        w2_sb = shared.tile([P, PASSES, 2 * H], U8, name="w2_sb", offset=20 * KIB, align_bytes=64)
+        w1s_dealt = keep.tile([P, PASSES, H], U8, name="w1s_dealt", align_bytes=64)
         intf_sb = [
             shared.tile([P, 2, S], F32, name="intf0", offset=4 * KIB, align_bytes=64),
             shared.tile([P, 2, S], F32, name="intf1", offset=16 * KIB, align_bytes=64),
         ]
         age_sb = [
-            shared.tile([P, 2, S], F32, name="age0", offset=11 * KIB, align_bytes=64),
-            shared.tile([P, 2, S], F32, name="age1", offset=20 * KIB, align_bytes=64),
+            shared.tile([P, 2, S], F32, name="age0", offset=8 * KIB, align_bytes=64),
+            shared.tile([P, 2, S], F32, name="age1", offset=23 * KIB, align_bytes=64),
         ]
         w1_raw = keep.tile([P, PASSES, 2 * H], U8, name="w1_raw")
         w1_dealt = keep.tile([P, PASSES, 2 * H], U8, name="w1_dealt", align_bytes=64)
-        w1s_raw = shared.tile([P, PASSES, H], U8, name="w1s_raw", offset=24 * KIB, align_bytes=64)
-        w2s_sb = keep.tile([P, PASSES, H], U8, name="w2s_sb", align_bytes=64)
+        w1s_raw = keep.tile([P, PASSES, H], U8, name="w1s_raw")
+        w2s_sb = shared.tile([P, PASSES, H], U8, name="w2s_sb", offset=22 * KIB, align_bytes=64)
         w3_sb = keep.tile([P, 2 * N], U8, name="w3_sb", align_bytes=64)
         w3s_sb = keep.tile([P, 1, N], U8, name="w3s_sb", align_bytes=64)
         unit_sb = keep.tile([P, PACK], F32, name="unit_sb")
         ident = keep.tile([P, P], F32, name="ident")
         windows = [keep.tile([P, WINDOW], F32, name=f"window{t}") for t in range(PACK)]
 
-        nc.vector.memset(w1s_raw[:].bitcast(I32), 0)
-        nc.vector.memset(xs_table[:].bitcast(I32), 0)
-        nc.vector.memset(w2s_sb[:].bitcast(I32), 0)
+        x_planes = keep.tile([P, PASSES, S], U8, name="x_planes", align_bytes=64)
+        nc.gpsimd.memset(w1s_raw[:].bitcast(I32), 0)
+        nc.vector.memset(windows[0][:, S:], 0.0)
+        nc.vector.memset(xs_table[32:64].bitcast(I32), 0)
+        nc.vector.memset(xs_table[64:P].bitcast(I32), 0)
+        nc.vector.memset(x_planes[:].bitcast(I32), 0)
         nc.vector.memset(w3s_sb[:].bitcast(I32), 0)
-        for t in range(PACK):
+        for t in range(1, 3):
             nc.vector.memset(windows[t][:, S:], 0.0)
+        nc.vector.memset(windows[3][:, S:], 0.0)
 
+        warm = keep.tile([P, 8], F32, name="warm")
+        nc.scalar.activation(warm[:], windows[0][:, S : S + 8], ACT.Exp)
         nc.sync.dma_start(offs_sb[:], offs)
-        for o in range(PASSES):
-            load_words(nc.sync, x_table[o][:], x_words[o].rearrange("p c r -> p (c r)"))
+        nc.sync.dma_start(out=xs_table[0:32].bitcast(I32), in_=x_scales.rearrange("o g c -> g o c").bitcast(I32))
+        load_words(nc.sync, x_table[0][:], x_words[0].rearrange("p c r -> p (c r)"))
+        load_scale_rows(nc.sync, w1s_raw, w1_scales)
+        load_words(nc.sync, w1_raw[:], w1_words.rearrange("o p b -> p o b"))
+        load_words(nc.sync, x_table[1][:], x_words[1].rearrange("p c r -> p (c r)"))
         nc.sync.dma_start(off_sb[:], off)
-        load_scale_rows(nc.sync, xs_table, x_scales)
-        load_scale_rows(nc.sync, w2s_sb, w2_scales)
-        load_words(nc.gpsimd, w1_raw[:], w1_words.rearrange("o p b -> p o b"))
-        load_scale_rows(nc.gpsimd, w1s_raw, w1_scales)
         make_identity(nc, ident[:])
         nc.gpsimd.dma_start(out=unit_sb[:], in_=unit.rearrange("(p t) o -> p (t o)", t=PACK))
         load_words(nc.gpsimd, w3_sb[:], w3_words[0])
         load_scale_rows(nc.gpsimd, w3s_sb, w3_scales)
 
+        xs_picked = keep.tile([P, S], U8, name="xs_picked")
+        nc.vector.tensor_copy(xs_picked[:], xs_table[:].indirect(offs_sb[:]))
+        for q in range(QUADS):
+            nc.scalar.dma_start(
+                out=x_planes[32 * q : 32 * q + 4].bitcast(I32), in_=xs_picked[8 * q : 8 * q + 8].bitcast(I32)
+            )
         nc.scalar.copy(
             out=w1_dealt[:].bitcast(U16).rearrange("p o (t m) -> p o t m", t=PACK),
             in_=w1_raw[:].bitcast(U16).rearrange("p o (m t) -> p o t m", t=PACK),
         )
-        x_codes = [
-            keep.tile([P, S], U32, name="x_codes0", align_bytes=64),
-            shared.tile([P, S], U32, name="x_codes1", offset=24 * KIB, align_bytes=64),
-        ]
-        x_plane = [keep.tile([P, S], U8, name=f"x_plane{o}", align_bytes=64) for o in range(PASSES)]
-        for o in range(PASSES):
-            nc.vector.tensor_copy(x_plane[o][:], xs_table[:, o, :].indirect(offs_sb[:]))
+        x_codes = [keep.tile([P, S], U32, name=f"x_codes{o}", align_bytes=64) for o in range(PASSES)]
+        x_plane = [x_planes[:, o, :] for o in range(PASSES)]
         nc.vector.tensor_copy(x_codes[0][:], x_table[0][:].bitcast(U32).indirect(offs_sb[:]))
         nc.vector.tensor_copy(
             out=w1s_dealt[:].rearrange("p o (t m) -> p o t m", t=PACK),
@@ -110,10 +116,13 @@ def tile_picked_yarpsd_str_p_kernel(
         )
         nc.vector.tensor_copy(x_codes[1][:], x_table[1][:].bitcast(U32).indirect(offs_sb[:]))
 
-        load_words(nc.sync, w2_sb[:], w2_words.rearrange("o p b -> p o b"))
         for h in range(2):
             nc.sync.dma_start(out=intf_sb[h][:], in_=intf.rearrange("(p t) j -> p t j", t=PACK)[:, 2 * h : 2 * h + 2, :])
             nc.sync.dma_start(out=age_sb[h][:], in_=age.rearrange("(p t) j -> p t j", t=PACK)[:, 2 * h : 2 * h + 2, :])
+
+        load_words(nc.sync, w2_sb[:], w2_words.rearrange("o p b -> p o b"))
+        nc.vector.memset(w2s_sb[:].bitcast(I32), 0)
+        load_scale_rows(nc.sync, w2s_sb, w2_scales)
 
         di = [psum.tile([P, S], F32, name=f"di{t}", tag=f"tile_bank{t}") for t in range(PACK)]
         for o, t in [(0, 0), (0, 1), (1, 0), (1, 1), (0, 2), (1, 2), (0, 3), (1, 3)]:
@@ -122,7 +131,7 @@ def tile_picked_yarpsd_str_p_kernel(
                 lhsT=w1_dealt[:, o, 2 * P * t : 2 * P * (t + 1)].bitcast(FP4X4),
                 lhsT_scale=w1s_dealt[:, o, P * t : P * (t + 1)],
                 rhs=x_codes[o][:].bitcast(FP8X4),
-                rhs_scale=x_plane[o][:],
+                rhs_scale=x_plane[o],
                 start=(o == 0),
                 stop=(o == PASSES - 1),
             )
@@ -139,60 +148,75 @@ def tile_picked_yarpsd_str_p_kernel(
                     stop=(o == PASSES - 1),
                 )
 
+        grown = keep.tile([P, PACK, S], F32, name="grown")
         soft = keep.tile([P, PACK, S], F32, name="soft")
-        tanh_t = keep.tile([P, PACK, BLOCKS, P], F32, name="tanh_t")
         own = keep.tile([P, PACK, S], F32, name="own")
         other = keep.tile([P, PACK, S], F32, name="other")
-        strc_t = keep.tile([P, PACK, S], F32, name="strc_t")
         for t in range(PACK):
-            nc.scalar.activation(soft[:, t, :], di[t][:], ACT.Exp)
-        for u in range(BLOCKS):
-            nc.scalar.activation(tanh_t[:, :, u, :], qi_t[u][:].rearrange("j (p t) -> j t p", t=PACK), ACT.Tanh, scale=-1.0)
-        nc.vector.tensor_scalar(soft[:], soft[:], EXP_CAP, 1.0, ALU.min, ALU.add)
-        for h in range(2):
-            nc.vector.tensor_tensor(intf_sb[h][:], intf_sb[h][:], age_sb[h][:], ALU.mult)
+            nc.scalar.activation(grown[:, t, :], di[t][:], ACT.Exp)
+            nc.vector.tensor_scalar(grown[:, t, :], grown[:, t, :], EXP_CAP, 1.0, ALU.min, ALU.add)
         for t in range(PACK):
-            nc.scalar.activation(soft[:, t, :], soft[:, t, :], ACT.Ln, scale=math.exp(0.2))
+            intf_age = intf_sb[t // 2][:, t % 2, :]
+            nc.vector.tensor_tensor(intf_age, intf_age, age_sb[t // 2][:, t % 2, :], ALU.mult)
+        for t in range(PACK):
+            nc.scalar.activation(soft[:, t, :], grown[:, t, :], ACT.Ln, scale=math.exp(0.2))
         for t in range(PACK):
             nc.vector.scalar_tensor_tensor(windows[t][:, :S], di[t][:], 0.2, soft[:, t, :], ALU.add, ALU.max)
-        for t in range(1, PACK):
-            nc.scalar.activation(other[:, t, :], windows[t][:].indirect(off_sb[:]), ACT.Copy)
+        nc.scalar.activation(other[:, 1, :], windows[1][:].indirect(off_sb[:]), ACT.Copy)
+        tanh_t = grown
+        for u in range(BLOCKS):
+            nc.scalar.activation(tanh_t[:, u, :], qi_t[u][:], ACT.Tanh, scale=-1.0)
 
-        def add_transposed(bank, first, second):
-            for n, src in enumerate((first, second)):
-                for u in range(BLOCKS):
-                    nc.tensor.matmul(
-                        bank[:, P * u : P * (u + 1)],
-                        src[:, P * u : P * (u + 1)],
-                        ident[:],
-                        is_transpose=True,
-                        start=(n == 0 and u == 0),
-                        stop=(n == 1 and u == BLOCKS - 1),
-                    )
+        def add_transposed(bank, blocks, start, stop):
+            for u in range(BLOCKS):
+                nc.tensor.matmul(
+                    bank[:, P * u : P * (u + 1)],
+                    blocks[u],
+                    ident[:],
+                    is_transpose=True,
+                    start=(start and u == 0),
+                    stop=(stop and u == BLOCKS - 1),
+                )
 
-        args = {}
+        def blocks_of(rows):
+            return [rows[:, P * u : P * (u + 1)] for u in range(BLOCKS)]
+
+        def tanh_blocks(t):
+            return [tanh_t[:, u, t:H:PACK] for u in range(BLOCKS)]
+
+        z_t = []
         for t in range(PACK):
             intf_age = intf_sb[t // 2][:, t % 2, :]
             nc.vector.tensor_tensor(own[:, t, :], windows[t][:, :S], age_sb[t // 2][:, t % 2, :], ALU.mult)
-            if t == 0:
+            if t != 1:
                 nc.vector.tensor_tensor(other[:, t, :], windows[t][:].indirect(off_sb[:]), intf_age, ALU.mult)
             else:
                 nc.vector.tensor_tensor(other[:, t, :], other[:, t, :], intf_age, ALU.mult)
-            z_t = psum.tile([P, S], F32, name=f"z_t{t}", tag=f"tile_bank{t}")
-            add_transposed(z_t, own[:, t, :], other[:, t, :])
-            nc.scalar.activation(strc_t[:, t, :], z_t[:], ACT.Sqrt, scale=0.5 / 0.81)
-        tanh_rows = [tanh_t[:, t].rearrange("j u p -> j (u p)") for t in range(PACK)]
-        for t, bank in [(1, 1), (2, 2), (0, 3), (3, 0)]:
-            arg = psum.tile([P, S], F32, name=f"arg{t}", tag=f"tile_bank{bank}")
-            add_transposed(arg, tanh_rows[t], strc_t[:, t, :])
-            args[t] = arg
-        rate = [soft[:, 0, :], strc_t[:, 0, :], tanh_rows[0], soft[:, 3, :]]
+            z_t.append(psum.tile([P, S], F32, name=f"z_t{t}", tag=f"tile_bank{t}"))
+            add_transposed(z_t[t], blocks_of(own[:, t, :]), True, False)
+            add_transposed(z_t[t], blocks_of(other[:, t, :]), False, True)
+        args = [psum.tile([P, S], F32, name=f"arg{t}", tag=f"block_bank{t}") for t in range(PACK)]
+        for t in range(PACK - 1):
+            add_transposed(args[t], tanh_blocks(t), True, False)
+        strc_t = [other[:, 1, :], other[:, 2, :], other[:, 3, :], own[:, 3, :]]
         for t in range(PACK):
-            nc.scalar.activation(rate[t], args[t][:], ACT.Exp, scale=-0.9)
-            if t == 0:
-                nc.vector.tensor_scalar(windows[t][:, :S], rate[t], unit_sb[:, t : t + 1], -0.4, ALU.mult, ALU.mult)
-                nc.vector.tensor_copy(other[:, t, :], windows[t][:].indirect(off_sb[:]))
-            nc.vector.tensor_scalar(own[:, t, :], rate[t], unit_sb[:, t : t + 1], None, ALU.mult)
+            nc.scalar.activation(strc_t[t], z_t[t][:], ACT.Sqrt, scale=0.5 / 0.81)
+            last = t == PACK - 1
+            add_transposed(args[t], blocks_of(strc_t[t]), last, not last)
+        add_transposed(args[PACK - 1], tanh_blocks(PACK - 1), False, True)
+        rate = grown
+        for t in range(PACK):
+            nc.scalar.activation(rate[:, t, :], args[t][:], ACT.Exp, scale=-0.9)
+
+        def times_unit(t):
+            nc.vector.tensor_scalar(own[:, t, :], rate[:, t, :], unit_sb[:, t : t + 1], None, ALU.mult)
+
+        nc.vector.tensor_scalar(windows[0][:, :S], rate[:, 0, :], unit_sb[:, 0:1], -0.4, ALU.mult, ALU.mult)
+        for h in range(2):
+            nc.vector.tensor_copy(other[:, 0, 256 * h : 256 * (h + 1)], windows[0][:].indirect(off_sb[:, 16 * h : 16 * (h + 1)]))
+            times_unit(h + 1)
+        times_unit(3)
+        times_unit(0)
 
         cw = S // CHUNKS
         hid = keep.tile([P, S, PACK], BF16, name="hid", align_bytes=64)
@@ -215,7 +239,7 @@ def tile_picked_yarpsd_str_p_kernel(
                 scales=hid_plane[:, cols],
                 in_=hid[:, cols, :].rearrange("p j t -> p (j t)"),
             )
-            acc = psum.tile([P, N // P, cw], F32, name=f"acc{c}", tag=f"block_bank{c}")
+            acc = psum.tile([P, N // P, cw], F32, name=f"acc{c}", tag=f"tile_bank{c}")
             for m in range(N // P):
                 nc.tensor.matmul_mx(
                     out=acc[:, m, :],
@@ -226,5 +250,5 @@ def tile_picked_yarpsd_str_p_kernel(
                     start=True,
                     stop=True,
                 )
-            nc.vector.tensor_copy(out=staged[:, :, cols], in_=acc[:])
+            nc.scalar.copy(out=staged[:, :, cols], in_=acc[:])
             nc.sync.dma_start(out=out.rearrange("(m p) j -> p m j", p=P)[:, :, cols], in_=staged[:, :, cols])

@@ -60,14 +60,14 @@ def tile_picked_yarpsd_str_p_kernel(
         ]
         age_sb = [
             shared.tile([P, 2, S], F32, name="age0", offset=8 * KIB, align_bytes=64),
-            shared.tile([P, 2, S], F32, name="age1", offset=23 * KIB, align_bytes=64),
+            shared.tile([P, 2, S], F32, name="age1", offset=23 * KIB + 768, align_bytes=64),
         ]
         w1_raw = keep.tile([P, PASSES, 2 * H], U8, name="w1_raw")
         w1_dealt = keep.tile([P, PASSES, 2 * H], U8, name="w1_dealt", align_bytes=64)
         w1s_raw = keep.tile([P, PASSES, H], U8, name="w1s_raw")
         w2s_sb = shared.tile([P, PASSES, H], U8, name="w2s_sb", offset=22 * KIB, align_bytes=64)
-        w3_sb = keep.tile([P, 2 * N], U8, name="w3_sb", align_bytes=64)
-        w3s_sb = keep.tile([P, 1, N], U8, name="w3s_sb", align_bytes=64)
+        w3_sb = shared.tile([P, 2 * N], U8, name="w3_sb", offset=23 * KIB, align_bytes=64)
+        w3s_sb = shared.tile([P, 1, N], U8, name="w3s_sb", offset=23 * KIB + 512, align_bytes=64)
         unit_sb = keep.tile([P, PACK], F32, name="unit_sb")
         ident = keep.tile([P, P], F32, name="ident")
         windows = [keep.tile([P, WINDOW], F32, name=f"window{t}") for t in range(PACK)]
@@ -78,24 +78,18 @@ def tile_picked_yarpsd_str_p_kernel(
         nc.vector.memset(xs_table[32:64].bitcast(I32), 0)
         nc.vector.memset(xs_table[64:P].bitcast(I32), 0)
         nc.vector.memset(x_planes[:].bitcast(I32), 0)
-        nc.vector.memset(w3s_sb[:].bitcast(I32), 0)
-        for t in range(1, 3):
-            nc.vector.memset(windows[t][:, S:], 0.0)
-        nc.vector.memset(windows[3][:, S:], 0.0)
+        for t in range(1, PACK):
+            nc.scalar.copy(windows[t][:, S:], windows[0][:, S:])
 
-        warm = keep.tile([P, 8], F32, name="warm")
-        nc.scalar.activation(warm[:], windows[0][:, S : S + 8], ACT.Exp)
         nc.sync.dma_start(offs_sb[:], offs)
         nc.sync.dma_start(out=xs_table[0:32].bitcast(I32), in_=x_scales.rearrange("o g c -> g o c").bitcast(I32))
+        nc.sync.dma_start(off_sb[:], off)
+        nc.sync.dma_start(out=unit_sb[:], in_=unit.rearrange("(p t) o -> p (t o)", t=PACK))
         load_words(nc.sync, x_table[0][:], x_words[0].rearrange("p c r -> p (c r)"))
-        load_scale_rows(nc.sync, w1s_raw, w1_scales)
         load_words(nc.sync, w1_raw[:], w1_words.rearrange("o p b -> p o b"))
         load_words(nc.sync, x_table[1][:], x_words[1].rearrange("p c r -> p (c r)"))
-        nc.sync.dma_start(off_sb[:], off)
+        load_scale_rows(nc.scalar, w1s_raw, w1_scales)
         make_identity(nc, ident[:])
-        nc.gpsimd.dma_start(out=unit_sb[:], in_=unit.rearrange("(p t) o -> p (t o)", t=PACK))
-        load_words(nc.gpsimd, w3_sb[:], w3_words[0])
-        load_scale_rows(nc.gpsimd, w3s_sb, w3_scales)
 
         xs_picked = keep.tile([P, S], U8, name="xs_picked")
         nc.vector.tensor_copy(xs_picked[:], xs_table[:].indirect(offs_sb[:]))
@@ -116,16 +110,21 @@ def tile_picked_yarpsd_str_p_kernel(
         )
         nc.vector.tensor_copy(x_codes[1][:], x_table[1][:].bitcast(U32).indirect(offs_sb[:]))
 
-        for h in range(2):
-            nc.sync.dma_start(out=intf_sb[h][:], in_=intf.rearrange("(p t) j -> p t j", t=PACK)[:, 2 * h : 2 * h + 2, :])
-            nc.sync.dma_start(out=age_sb[h][:], in_=age.rearrange("(p t) j -> p t j", t=PACK)[:, 2 * h : 2 * h + 2, :])
+        def load_factors(h):
+            for tile, rows in ((intf_sb[h], intf), (age_sb[h], age)):
+                nc.sync.dma_start(out=tile[:], in_=rows.rearrange("(p t) j -> p t j", t=PACK)[:, 2 * h : 2 * h + 2, :])
 
-        load_words(nc.sync, w2_sb[:], w2_words.rearrange("o p b -> p o b"))
+        load_factors(0)
         nc.vector.memset(w2s_sb[:].bitcast(I32), 0)
+        nc.vector.memset(w3s_sb[:].bitcast(I32), 0)
+        load_words(nc.sync, w2_sb[:], w2_words.rearrange("o p b -> p o b"))
         load_scale_rows(nc.sync, w2s_sb, w2_scales)
+        load_factors(1)
+        load_words(nc.sync, w3_sb[:], w3_words[0])
+        load_scale_rows(nc.sync, w3s_sb, w3_scales)
 
         di = [psum.tile([P, S], F32, name=f"di{t}", tag=f"tile_bank{t}") for t in range(PACK)]
-        for o, t in [(0, 0), (0, 1), (1, 0), (1, 1), (0, 2), (1, 2), (0, 3), (1, 3)]:
+        for o, t in [(0, 0), (0, 1), (0, 2), (1, 0), (1, 1), (1, 2), (0, 3), (1, 3)]:
             nc.tensor.matmul_mx(
                 out=di[t][:],
                 lhsT=w1_dealt[:, o, 2 * P * t : 2 * P * (t + 1)].bitcast(FP4X4),
@@ -157,7 +156,8 @@ def tile_picked_yarpsd_str_p_kernel(
             nc.vector.tensor_scalar(grown[:, t, :], grown[:, t, :], EXP_CAP, 1.0, ALU.min, ALU.add)
         for t in range(PACK):
             intf_age = intf_sb[t // 2][:, t % 2, :]
-            nc.vector.tensor_tensor(intf_age, intf_age, age_sb[t // 2][:, t % 2, :], ALU.mult)
+            engine = nc.vector if t < 2 else nc.gpsimd
+            engine.tensor_tensor(intf_age, intf_age, age_sb[t // 2][:, t % 2, :], ALU.mult)
         for t in range(PACK):
             nc.scalar.activation(soft[:, t, :], grown[:, t, :], ACT.Ln, scale=math.exp(0.2))
         for t in range(PACK):
@@ -165,7 +165,12 @@ def tile_picked_yarpsd_str_p_kernel(
         nc.scalar.activation(other[:, 1, :], windows[1][:].indirect(off_sb[:]), ACT.Copy)
         tanh_t = grown
         for u in range(BLOCKS):
-            nc.scalar.activation(tanh_t[:, u, :], qi_t[u][:], ACT.Tanh, scale=-1.0)
+            nc.scalar.activation(
+                tanh_t[:, :, P * u : P * (u + 1)].rearrange("j t p -> j p t"),
+                qi_t[u][:].rearrange("j (p t) -> j p t", t=PACK),
+                ACT.Tanh,
+                scale=-1.0,
+            )
 
         def add_transposed(bank, blocks, start, stop):
             for u in range(BLOCKS):
@@ -182,7 +187,7 @@ def tile_picked_yarpsd_str_p_kernel(
             return [rows[:, P * u : P * (u + 1)] for u in range(BLOCKS)]
 
         def tanh_blocks(t):
-            return [tanh_t[:, u, t:H:PACK] for u in range(BLOCKS)]
+            return blocks_of(tanh_t[:, t, :])
 
         z_t = []
         for t in range(PACK):
@@ -195,28 +200,32 @@ def tile_picked_yarpsd_str_p_kernel(
             z_t.append(psum.tile([P, S], F32, name=f"z_t{t}", tag=f"tile_bank{t}"))
             add_transposed(z_t[t], blocks_of(own[:, t, :]), True, False)
             add_transposed(z_t[t], blocks_of(other[:, t, :]), False, True)
-        args = [psum.tile([P, S], F32, name=f"arg{t}", tag=f"block_bank{t}") for t in range(PACK)]
-        for t in range(PACK - 1):
-            add_transposed(args[t], tanh_blocks(t), True, False)
         strc_t = [other[:, 1, :], other[:, 2, :], other[:, 3, :], own[:, 3, :]]
+        arg_bank = ["block_bank0", "tile_bank2", "tile_bank3", "block_bank3"]
+        args = {}
+
+        def exponent(t):
+            args[t] = psum.tile([P, S], F32, name=f"arg{t}", tag=arg_bank[t])
+            add_transposed(args[t], blocks_of(strc_t[t]), True, False)
+            add_transposed(args[t], tanh_blocks(t), False, True)
+
         for t in range(PACK):
             nc.scalar.activation(strc_t[t], z_t[t][:], ACT.Sqrt, scale=0.5 / 0.81)
-            last = t == PACK - 1
-            add_transposed(args[t], blocks_of(strc_t[t]), last, not last)
-        add_transposed(args[PACK - 1], tanh_blocks(PACK - 1), False, True)
-        rate = grown
+        for t in (0, 1, 3, 2):
+            exponent(t)
+        rate = [own[:, 3, :], tanh_t[:, 3, :], soft[:, 2, :], soft[:, 3, :]]
         for t in range(PACK):
-            nc.scalar.activation(rate[:, t, :], args[t][:], ACT.Exp, scale=-0.9)
+            nc.scalar.activation(rate[t], args[t][:], ACT.Exp, scale=-0.9)
 
         def times_unit(t):
-            nc.vector.tensor_scalar(own[:, t, :], rate[:, t, :], unit_sb[:, t : t + 1], None, ALU.mult)
+            nc.vector.tensor_scalar(own[:, t, :], rate[t], unit_sb[:, t : t + 1], None, ALU.mult)
 
-        nc.vector.tensor_scalar(windows[0][:, :S], rate[:, 0, :], unit_sb[:, 0:1], -0.4, ALU.mult, ALU.mult)
+        nc.vector.tensor_scalar(windows[0][:, :S], rate[0], unit_sb[:, 0:1], -0.4, ALU.mult, ALU.mult)
         for h in range(2):
             nc.vector.tensor_copy(other[:, 0, 256 * h : 256 * (h + 1)], windows[0][:].indirect(off_sb[:, 16 * h : 16 * (h + 1)]))
             times_unit(h + 1)
-        times_unit(3)
         times_unit(0)
+        times_unit(3)
 
         cw = S // CHUNKS
         hid = keep.tile([P, S, PACK], BF16, name="hid", align_bytes=64)

import math
from contextlib import ExitStack

import concourse.mybir as mybir
from concourse.masks import make_identity

K, T, S, N, H = 1024, 2048, 512, 256, 512
FLOPS = 2 * (2 * K * H * S + H * N * S)

F32, BF16 = mybir.dt.float32, mybir.dt.bfloat16
I32, U32, U16, U8 = mybir.dt.int32, mybir.dt.uint32, mybir.dt.uint16, mybir.dt.uint8
FP8X4, FP4X4 = mybir.dt.float8_e4m3fn_x4, mybir.dt.float4_e2m1fn_x4
ALU = mybir.AluOpType
ACT = mybir.ActivationFunctionType

P = 128
PACK = 4
PASSES = K // (P * PACK)
QUADS = 4
BLOCKS = S // P
WINDOW = 704
EXP_CAP = 2.0**56
CHUNKS = 4
KIB = 1024


def load_scale_rows(queue, plane, scales):
    for r in range(4):
        queue.dma_start(
            out=plane[r:P:32].bitcast(I32),
            in_=scales.rearrange("o (q r) c -> r q o c", r=4)[r].bitcast(I32),
        )


def load_words(queue, tile, words):
    queue.dma_start(out=tile.bitcast(I32), in_=words.bitcast(I32))


def tile_picked_yarpsd_str_p_kernel(
    tc, x_words, x_scales, w1_words, w1_scales, w2_words, w2_scales, intf, age, unit, w3_words, w3_scales, offs, off, out
):
    nc = tc.nc
    with ExitStack() as ctx:
        keep = ctx.enter_context(tc.tile_pool(name="keep", bufs=1))
        shared = ctx.enter_context(tc.tile_pool(name="shared", bufs=1))
        psum = ctx.enter_context(tc.psum_pool(name="psum", bufs=1))

        offs_sb = keep.tile([P, S // 16], U16, name="offs_sb")
        off_sb = keep.tile([P, S // 16], U16, name="off_sb")
        xs_table = shared.tile([P, T], U8, name="xs_table", offset=0, align_bytes=64)
        x_table = [
            shared.tile([P, T], I32, name="x_table0", offset=4 * KIB, align_bytes=64),
            shared.tile([P, T], I32, name="x_table1", offset=16 * KIB, align_bytes=64),
        ]
        w2_sb = shared.tile([P, PASSES, 2 * H], U8, name="w2_sb", offset=20 * KIB, align_bytes=64)
        w1s_dealt = keep.tile([P, PASSES, H], U8, name="w1s_dealt", align_bytes=64)
        intf_sb = [
            shared.tile([P, 2, S], F32, name="intf0", offset=4 * KIB, align_bytes=64),
            shared.tile([P, 2, S], F32, name="intf1", offset=16 * KIB, align_bytes=64),
        ]
        age_sb = [
            shared.tile([P, 2, S], F32, name="age0", offset=8 * KIB, align_bytes=64),
            shared.tile([P, 2, S], F32, name="age1", offset=23 * KIB + 768, align_bytes=64),
        ]
        w1_raw = keep.tile([P, PASSES, 2 * H], U8, name="w1_raw")
        w1_dealt = keep.tile([P, PASSES, 2 * H], U8, name="w1_dealt", align_bytes=64)
        w1s_raw = keep.tile([P, PASSES, H], U8, name="w1s_raw")
        w2s_sb = shared.tile([P, PASSES, H], U8, name="w2s_sb", offset=22 * KIB, align_bytes=64)
        w3_sb = shared.tile([P, 2 * N], U8, name="w3_sb", offset=23 * KIB, align_bytes=64)
        w3s_sb = shared.tile([P, 1, N], U8, name="w3s_sb", offset=23 * KIB + 512, align_bytes=64)
        unit_sb = keep.tile([P, PACK], F32, name="unit_sb")
        ident = keep.tile([P, P], F32, name="ident")
        windows = [keep.tile([P, WINDOW], F32, name=f"window{t}") for t in range(PACK)]

        x_planes = keep.tile([P, PASSES, S], U8, name="x_planes", align_bytes=64)
        nc.gpsimd.memset(w1s_raw[:].bitcast(I32), 0)
        nc.vector.memset(windows[0][:, S:], 0.0)
        nc.vector.memset(xs_table[32:64].bitcast(I32), 0)
        nc.vector.memset(xs_table[64:P].bitcast(I32), 0)
        nc.vector.memset(x_planes[:].bitcast(I32), 0)
        for t in range(1, PACK):
            nc.scalar.copy(windows[t][:, S:], windows[0][:, S:])

        nc.sync.dma_start(offs_sb[:], offs)
        nc.sync.dma_start(out=xs_table[0:32].bitcast(I32), in_=x_scales.rearrange("o g c -> g o c").bitcast(I32))
        nc.sync.dma_start(off_sb[:], off)
        nc.sync.dma_start(out=unit_sb[:], in_=unit.rearrange("(p t) o -> p (t o)", t=PACK))
        load_words(nc.sync, x_table[0][:], x_words[0].rearrange("p c r -> p (c r)"))
        load_words(nc.sync, w1_raw[:], w1_words.rearrange("o p b -> p o b"))
        load_words(nc.sync, x_table[1][:], x_words[1].rearrange("p c r -> p (c r)"))
        load_scale_rows(nc.scalar, w1s_raw, w1_scales)
        make_identity(nc, ident[:])

        xs_picked = keep.tile([P, S], U8, name="xs_picked")
        nc.vector.tensor_copy(xs_picked[:], xs_table[:].indirect(offs_sb[:]))
        for q in range(QUADS):
            nc.scalar.dma_start(
                out=x_planes[32 * q : 32 * q + 4].bitcast(I32), in_=xs_picked[8 * q : 8 * q + 8].bitcast(I32)
            )
        nc.scalar.copy(
            out=w1_dealt[:].bitcast(U16).rearrange("p o (t m) -> p o t m", t=PACK),
            in_=w1_raw[:].bitcast(U16).rearrange("p o (m t) -> p o t m", t=PACK),
        )
        x_codes = [keep.tile([P, S], U32, name=f"x_codes{o}", align_bytes=64) for o in range(PASSES)]
        x_plane = [x_planes[:, o, :] for o in range(PASSES)]
        nc.vector.tensor_copy(x_codes[0][:], x_table[0][:].bitcast(U32).indirect(offs_sb[:]))
        nc.vector.tensor_copy(
            out=w1s_dealt[:].rearrange("p o (t m) -> p o t m", t=PACK),
            in_=w1s_raw[:].rearrange("p o (m t) -> p o t m", t=PACK),
        )
        nc.vector.tensor_copy(x_codes[1][:], x_table[1][:].bitcast(U32).indirect(offs_sb[:]))

        def load_factors(h):
            for tile, rows in ((intf_sb[h], intf), (age_sb[h], age)):
                nc.sync.dma_start(out=tile[:], in_=rows.rearrange("(p t) j -> p t j", t=PACK)[:, 2 * h : 2 * h + 2, :])

        load_factors(0)
        nc.vector.memset(w2s_sb[:].bitcast(I32), 0)
        nc.vector.memset(w3s_sb[:].bitcast(I32), 0)
        load_words(nc.sync, w2_sb[:], w2_words.rearrange("o p b -> p o b"))
        load_scale_rows(nc.sync, w2s_sb, w2_scales)
        load_factors(1)
        load_words(nc.sync, w3_sb[:], w3_words[0])
        load_scale_rows(nc.sync, w3s_sb, w3_scales)

        di = [psum.tile([P, S], F32, name=f"di{t}", tag=f"tile_bank{t}") for t in range(PACK)]
        for o, t in [(0, 0), (0, 1), (0, 2), (1, 0), (1, 1), (1, 2), (0, 3), (1, 3)]:
            nc.tensor.matmul_mx(
                out=di[t][:],
                lhsT=w1_dealt[:, o, 2 * P * t : 2 * P * (t + 1)].bitcast(FP4X4),
                lhsT_scale=w1s_dealt[:, o, P * t : P * (t + 1)],
                rhs=x_codes[o][:].bitcast(FP8X4),
                rhs_scale=x_plane[o],
                start=(o == 0),
                stop=(o == PASSES - 1),
            )
        qi_t = [psum.tile([P, H], F32, name=f"qi_t{u}", tag=f"block_bank{u}") for u in range(BLOCKS)]
        for u in range(BLOCKS):
            for o in range(PASSES):
                nc.tensor.matmul_mx(
                    out=qi_t[u][:],
                    lhsT=x_codes[o][:, P * u : P * (u + 1)].bitcast(FP8X4),
                    lhsT_scale=x_plane[o][:, P * u : P * (u + 1)],
                    rhs=w2_sb[:, o, :].bitcast(FP4X4),
                    rhs_scale=w2s_sb[:, o, :],
                    start=(o == 0),
                    stop=(o == PASSES - 1),
                )

        grown = keep.tile([P, PACK, S], F32, name="grown")
        soft = keep.tile([P, PACK, S], F32, name="soft")
        own = keep.tile([P, PACK, S], F32, name="own")
        other = keep.tile([P, PACK, S], F32, name="other")
        for t in range(PACK):
            nc.scalar.activation(grown[:, t, :], di[t][:], ACT.Exp)
            nc.vector.tensor_scalar(grown[:, t, :], grown[:, t, :], EXP_CAP, 1.0, ALU.min, ALU.add)
        for t in range(PACK):
            intf_age = intf_sb[t // 2][:, t % 2, :]
            engine = nc.vector if t < 2 else nc.gpsimd
            engine.tensor_tensor(intf_age, intf_age, age_sb[t // 2][:, t % 2, :], ALU.mult)
        for t in range(PACK):
            nc.scalar.activation(soft[:, t, :], grown[:, t, :], ACT.Ln, scale=math.exp(0.2))
        for t in range(PACK):
            nc.vector.scalar_tensor_tensor(windows[t][:, :S], di[t][:], 0.2, soft[:, t, :], ALU.add, ALU.max)
        nc.scalar.activation(other[:, 1, :], windows[1][:].indirect(off_sb[:]), ACT.Copy)
        tanh_t = grown
        for u in range(BLOCKS):
            nc.scalar.activation(
                tanh_t[:, :, P * u : P * (u + 1)].rearrange("j t p -> j p t"),
                qi_t[u][:].rearrange("j (p t) -> j p t", t=PACK),
                ACT.Tanh,
                scale=-1.0,
            )

        def add_transposed(bank, blocks, start, stop):
            for u in range(BLOCKS):
                nc.tensor.matmul(
                    bank[:, P * u : P * (u + 1)],
                    blocks[u],
                    ident[:],
                    is_transpose=True,
                    start=(start and u == 0),
                    stop=(stop and u == BLOCKS - 1),
                )

        def blocks_of(rows):
            return [rows[:, P * u : P * (u + 1)] for u in range(BLOCKS)]

        def tanh_blocks(t):
            return blocks_of(tanh_t[:, t, :])

        z_t = []
        for t in range(PACK):
            intf_age = intf_sb[t // 2][:, t % 2, :]
            nc.vector.tensor_tensor(own[:, t, :], windows[t][:, :S], age_sb[t // 2][:, t % 2, :], ALU.mult)
            if t != 1:
                nc.vector.tensor_tensor(other[:, t, :], windows[t][:].indirect(off_sb[:]), intf_age, ALU.mult)
            else:
                nc.vector.tensor_tensor(other[:, t, :], other[:, t, :], intf_age, ALU.mult)
            z_t.append(psum.tile([P, S], F32, name=f"z_t{t}", tag=f"tile_bank{t}"))
            add_transposed(z_t[t], blocks_of(own[:, t, :]), True, False)
            add_transposed(z_t[t], blocks_of(other[:, t, :]), False, True)
        strc_t = [other[:, 1, :], other[:, 2, :], other[:, 3, :], own[:, 3, :]]
        arg_bank = ["block_bank0", "tile_bank2", "tile_bank3", "block_bank3"]
        args = {}

        def exponent(t):
            args[t] = psum.tile([P, S], F32, name=f"arg{t}", tag=arg_bank[t])
            add_transposed(args[t], blocks_of(strc_t[t]), True, False)
            add_transposed(args[t], tanh_blocks(t), False, True)

        for t in range(PACK):
            nc.scalar.activation(strc_t[t], z_t[t][:], ACT.Sqrt, scale=0.5 / 0.81)
        for t in (0, 1, 3, 2):
            exponent(t)
        rate = [own[:, 3, :], tanh_t[:, 3, :], soft[:, 2, :], soft[:, 3, :]]
        for t in range(PACK):
            nc.scalar.activation(rate[t], args[t][:], ACT.Exp, scale=-0.9)

        def times_unit(t):
            nc.vector.tensor_scalar(own[:, t, :], rate[t], unit_sb[:, t : t + 1], None, ALU.mult)

        nc.vector.tensor_scalar(windows[0][:, :S], rate[0], unit_sb[:, 0:1], -0.4, ALU.mult, ALU.mult)
        for h in range(2):
            nc.vector.tensor_copy(other[:, 0, 256 * h : 256 * (h + 1)], windows[0][:].indirect(off_sb[:, 16 * h : 16 * (h + 1)]))
            times_unit(h + 1)
        times_unit(0)
        times_unit(3)

        cw = S // CHUNKS
        hid = keep.tile([P, S, PACK], BF16, name="hid", align_bytes=64)
        hid_codes = keep.tile([P, S], U32, name="hid_codes", align_bytes=64)
        hid_plane = keep.tile([P, S], U8, name="hid_plane", align_bytes=64)
        staged = keep.tile([P, N // P, S], F32, name="staged")
        for c in range(CHUNKS):
            cols = slice(c * cw, (c + 1) * cw)
            entries = off_sb[:, c * cw // 16 : (c + 1) * cw // 16]
            for t in range(1, PACK):
                nc.scalar.activation(other[:, t, cols], own[:, t, :].indirect(entries), ACT.Copy, scale=-0.4)
            nc.vector.tensor_tensor(
                hid[:, cols, :].rearrange("p (c i) t -> p c t i", i=4),
                other[:, :, cols].rearrange("p t (c i) -> p c t i", i=4),
                own[:, :, cols].rearrange("p t (c i) -> p c t i", i=4),
                ALU.add,
            )
            nc.vector.quantize_mx(
                out=hid_codes[:, cols].bitcast(FP8X4),
                scales=hid_plane[:, cols],
                in_=hid[:, cols, :].rearrange("p j t -> p (j t)"),
            )
            acc = psum.tile([P, N // P, cw], F32, name=f"acc{c}", tag=f"tile_bank{c}")
            for m in range(N // P):
                nc.tensor.matmul_mx(
                    out=acc[:, m, :],
                    lhsT=w3_sb[:, 2 * P * m : 2 * P * (m + 1)].bitcast(FP4X4),
                    lhsT_scale=w3s_sb[:, 0, P * m : P * (m + 1)],
                    rhs=hid_codes[:, cols].bitcast(FP8X4),
                    rhs_scale=hid_plane[:, cols],
                    start=True,
                    stop=True,
                )
            nc.scalar.copy(out=staged[:, :, cols], in_=acc[:])
            nc.sync.dma_start(out=out.rearrange("(m p) j -> p m j", p=P)[:, :, cols], in_=staged[:, :, cols])
